import numpy as np
import ml_dtypes


def mxq(x, axis, fmt="e4m3"):
    dtype, down = {"e4m3": (ml_dtypes.float8_e4m3fn, 7), "e5m2": (ml_dtypes.float8_e5m2, 14)}[fmt]
    v = np.moveaxis(np.asarray(x, np.float32).astype(ml_dtypes.bfloat16).astype(np.float64), axis, -1)
    blocks = v.reshape(v.shape[:-1] + (-1, 32))
    amax = np.abs(blocks).max(-1, keepdims=True)
    byte = np.maximum(np.where(amax > 0, np.frexp(amax)[1] - 1 + 127, 0) - down, 1)
    scale = np.exp2(byte - 127.0)
    codes = (blocks / scale).astype(np.float32).astype(dtype).astype(np.float64)
    return np.moveaxis((codes * scale).reshape(v.shape), -1, axis)


WIDE = False


def mx_kscale(k):
    if not WIDE:
        return np.ones(k)
    levels = np.array([10, -10, 5, -5, 0])
    if k % 512:
        return np.exp2(np.random.permutation(np.resize(levels, k // 32))).repeat(32)
    a = np.empty((k // 512, 16))
    for p in range(k // 512):
        a[p, :8] = np.random.permutation(np.resize(levels, 8))
        for g in range(8):
            far = levels[np.abs(levels - a[p, g]) >= 10]
            a[p, g + 8] = far[np.random.randint(len(far))]
    return np.exp2(a.ravel()).repeat(32)


def f64(x):
    return np.asarray(x).astype(np.float64)


def striped(idx):
    return np.tile(idx.reshape(-1, 16).T, (8, 1)).astype(np.uint16)


def unstriped(offs):
    return offs[:16].T.reshape(-1).astype(np.int64)


def striped8(idx):
    return np.concatenate([x.reshape(-1, 16).T for x in idx]).astype(np.uint16)


def runs(offs, k):
    lists = np.stack([offs[16 * r : 16 * r + 16].T.reshape(-1) for r in range(8)]).astype(np.int64)
    return lists[np.arange(k) % 512 // 64]


def pack_weight(w):
    k, n = w.shape
    w = f64(np.asarray(w, np.float32).astype(ml_dtypes.bfloat16)).reshape(k // 32, 32, n)
    amax = np.abs(w).max(1)
    byte = np.clip(np.where(amax > 0, np.frexp(amax)[1] - 1 + 127 - 7, 1), 1, 254)
    scaled = (w * np.exp2(127.0 - byte)[:, None, :]).reshape(k, n).astype(np.float32)
    words = np.ascontiguousarray(scaled.reshape(k // 512, 128, 4, n).transpose(0, 1, 3, 2)).astype(ml_dtypes.float8_e4m3fn).view(np.uint8)
    return words, np.ascontiguousarray(byte.astype(np.uint8).reshape(k // 512, 16, n))


def unpack_weight(words, scales):
    g, p, n, _ = words.shape
    vals = np.ascontiguousarray(words).view(ml_dtypes.float8_e4m3fn).astype(np.float64) * np.repeat(np.exp2(scales.astype(np.float64) - 127.0), 8, axis=1)[..., None]
    return vals.transpose(0, 1, 3, 2).reshape(g * 512, n)

def planes(y):
    n, m = y.shape
    v = y.astype(np.float32).astype(ml_dtypes.bfloat16).astype(np.float64).reshape(n // 32, 32, m)
    top = np.abs(v).max(1)
    byte = np.clip(np.where(top > 0, np.frexp(top)[1] - 1 + 127 - 7, 1), 1, 254)
    codes = (v * np.exp2(127.0 - byte)[:, None, :]).reshape(n, m).astype(np.float32).astype(ml_dtypes.float8_e4m3fn).view(np.uint8)
    words = codes.reshape(n // 512, 128, 4, m).transpose(0, 1, 3, 2)
    return np.ascontiguousarray(words), np.ascontiguousarray(byte.astype(np.uint8).reshape(n // 512, 16, m))


K, T, S, N, G, H = 512, 2048, 512, 512, 2048, 512


def setup_inputs():
    n = np.random.standard_normal
    s = mx_kscale(K)[:, None]
    u = mx_kscale(S)
    packed_xT = pack_weight(n((K, T)) * s)
    packed_dT = pack_weight(n((K, G)) / s)
    packed_w1 = pack_weight(n((H, N)) / np.sqrt(H) / u[:, None])
    return {
        "x_words": packed_xT[0],
        "x_scales": packed_xT[1],
        "d_words": packed_dT[0],
        "d_scales": packed_dT[1],
        "gn": (np.random.uniform(0.5, 1.5, (H, 1)) * u[:, None]).astype(np.float32),
        "w1_words": packed_w1[0],
        "w1_scales": packed_w1[1],
        "offs": striped8(np.random.randint(0, T, (8, S))),
        "k1": striped8(np.random.randint(0, G, (8, H))),
        "n1": striped8(np.stack([np.random.permutation(S) for _ in range(8)])),
        "n2": striped(np.random.permutation(S)),
        "n3": striped(np.random.permutation(S)),
    }


def reference(x_words, x_scales, d_words, d_scales, gn, w1_words, w1_scales, offs, k1, n1, n2, n3):
    d_k1 = unpack_weight(d_words, d_scales)[np.arange(K)[:, None], runs(k1, K)]
    xq = unpack_weight(x_words, x_scales)[np.arange(K)[:, None], runs(offs, K)]
    h = 0.0625 * (d_k1.T @ xq)
    st = h - (h[np.arange(H)[:, None], runs(n1, H)])
    z = f64(gn) * (st - (0.5 * (st[np.arange(H)[:, None], runs(n1, H)])))
    h2 = unpack_weight(w1_words, w1_scales).T @ mxq(z, 0, "e4m3")
    ex = np.exp(0.5 * h2)
    out_0 = (2.0 * ex) / (ex + ex[:, unstriped(n2)] + ex[:, unstriped(n3)])
    return (out_0,) + planes(out_0)

@@ -1,0 +1,246 @@
+from contextlib import ExitStack
+
+import concourse.mybir as mybir
+
+K, T, S, N, G, H = 512, 2048, 512, 512, 2048, 512
+FLOPS = 2 * K * H * S + 2 * H * N * S
+
+F32 = mybir.dt.float32
+BF16 = mybir.dt.bfloat16
+I32 = mybir.dt.int32
+U32 = mybir.dt.uint32
+U16 = mybir.dt.uint16
+U8 = mybir.dt.uint8
+FP8X4 = mybir.dt.float8_e4m3fn_x4
+ALU = mybir.AluOpType
+ACT = mybir.ActivationFunctionType
+
+P = 128
+PACK = 4
+HALF = S // 2
+
+
+def tile_picked_hpqtwiceshare_none_po_kernel(
+    tc, x_words, x_scales, d_words, d_scales, gn, w1_words, w1_scales, offs, k1, n1, n2, n3, out_0, out_1, out_2
+):
+    nc = tc.nc
+    halves = [slice(0, HALF), slice(HALF, S)]
+
+    def entries(lst, cols):
+        return lst[:, cols.start // 16 : cols.stop // 16]
+
+    def gather(engine, out, window, offsets):
+        if engine == "vector":
+            nc.vector.tensor_copy(out=out, in_=window.indirect(offsets))
+        else:
+            nc.scalar.activation(out=out, in_=window.indirect(offsets), func=ACT.Copy)
+
+    def as_words(packed):
+        return packed[0].rearrange("p n t -> p (n t)").bitcast(I32)
+
+    with ExitStack() as ctx:
+        keep = ctx.enter_context(tc.tile_pool(name="keep", bufs=1))
+        psum = ctx.enter_context(tc.psum_pool(name="psum", bufs=1))
+
+        k1_list = keep.tile([P, H // 16], U16)
+        offs_list = keep.tile([P, S // 16], U16)
+        n1_list = keep.tile([P, S // 16], U16)
+        n2_list = keep.tile([P, S // 16], U16)
+        n3_list = keep.tile([P, S // 16], U16)
+        d_bytes = keep.tile([P, G], U8, align_bytes=64)
+        x_bytes = keep.tile([P, T], U8, align_bytes=64)
+        nc.sync.dma_start(k1_list[:], k1)
+        nc.sync.dma_start(d_bytes[:].bitcast(I32), d_scales[0].bitcast(I32).unsqueeze(1).broadcast_to([16, 8, G // 4]))
+        nc.sync.dma_start(offs_list[:], offs)
+        nc.sync.dma_start(x_bytes[:].bitcast(I32), x_scales[0].bitcast(I32).unsqueeze(1).broadcast_to([16, 8, T // 4]))
+        nc.sync.dma_start(n1_list[:], n1)
+        nc.sync.dma_start(n2_list[:], n2)
+
+        d_table = keep.tile([P, G], U32, align_bytes=64)
+        x_table = keep.tile([P, T], U32, align_bytes=64, tag="x_table")
+        w_table = keep.tile([P, N], U32, align_bytes=64)
+        nc.sync.dma_start(d_table[:].bitcast(I32), as_words(d_words))
+        nc.sync.dma_start(x_table[:].bitcast(I32), as_words(x_words))
+        nc.sync.dma_start(w_table[:].bitcast(I32), as_words(w1_words))
+        nc.sync.dma_start(n3_list[:], n3)
+
+        gain_raw = keep.tile([P, PACK], F32)
+        nc.gpsimd.dma_start(gain_raw[:], gn.rearrange("(p t) o -> p (t o)", t=PACK))
+        w_bytes = keep.tile([P, N], U8, align_bytes=64)
+        nc.gpsimd.memset(w_bytes[:].bitcast(I32), 0)
+        planes1 = keep.tile([P, H + S], U8, align_bytes=64)
+        nc.gpsimd.memset(planes1[:].bitcast(I32), 0)
+        for q in range(4):
+            nc.gpsimd.dma_start(
+                w_bytes[32 * q : 32 * q + 4, :].bitcast(I32), w1_scales[0, 4 * q : 4 * q + 4, :].bitcast(I32)
+            )
+        gain = keep.tile([P, PACK], F32)
+        nc.scalar.activation(out=gain[:], in_=gain_raw[:], func=ACT.Copy, scale=0.0625)
+
+        d_bytes_picked = keep.tile([P, H], U8, align_bytes=64)
+        x_bytes_picked = keep.tile([P, S], U8, align_bytes=64)
+        nc.vector.tensor_copy(out=d_bytes_picked[:], in_=d_bytes[:].indirect(k1_list[:]))
+        joined = keep.tile([P, H + S], U8, align_bytes=64)
+        nc.vector.tensor_copy(
+            out=joined[:, :H].rearrange("p (t m) -> p t m", t=PACK),
+            in_=d_bytes_picked[:].rearrange("p (m t) -> p t m", t=PACK),
+        )
+        nc.vector.tensor_copy(out=x_bytes_picked[:], in_=x_bytes[:].indirect(offs_list[:]))
+        nc.vector.tensor_copy(out=joined[:, H:].bitcast(I32), in_=x_bytes_picked[:].bitcast(I32))
+        for c in range(4):
+            nc.scalar.dma_start(planes1[c:P:32, :].bitcast(I32), joined[8 * c : P : 32, :].bitcast(I32))
+
+        d_picked = keep.tile([P, H], U32, align_bytes=64)
+        d_dealt = keep.tile([P, H], U32, align_bytes=64)
+        x_picked = keep.tile([P, S], U32, align_bytes=64)
+        nc.vector.tensor_copy(out=d_picked[:], in_=d_table[:].indirect(k1_list[:]))
+        nc.vector.tensor_copy(
+            out=d_dealt[:].rearrange("p (t c i) -> p c t i", t=PACK, i=4),
+            in_=d_picked[:].rearrange("p (c i t) -> p c t i", t=PACK, i=4),
+        )
+        for cols in halves:
+            nc.vector.tensor_copy(out=x_picked[:, cols], in_=x_table[:].indirect(entries(offs_list, cols)))
+
+        w_dealt = keep.tile([P, N], U32, align_bytes=64)
+        nc.scalar.copy(
+            out=w_dealt[:].rearrange("p (t c i) -> p c t i", t=PACK, i=4),
+            in_=w_table[:].rearrange("p (c i t) -> p c t i", t=PACK, i=4),
+        )
+        w_plane = keep.tile([P, N], U8, align_bytes=64, tag="x_table")
+        nc.vector.tensor_copy(
+            out=w_plane[:].rearrange("p (t m) -> p t m", t=PACK),
+            in_=w_bytes[:].rearrange("p (m t) -> p t m", t=PACK),
+        )
+
+        h_bank = [psum.tile([P, S], F32, name="h_bank%d" % t) for t in range(PACK)]
+        for t in range(PACK):
+            rows = slice(t * P, (t + 1) * P)
+            for cols in halves:
+                nc.tensor.matmul_mx(
+                    out=h_bank[t][:, cols],
+                    lhsT=d_dealt[:, rows].bitcast(FP8X4),
+                    lhsT_scale=planes1[:, rows],
+                    rhs=x_picked[:, cols].bitcast(FP8X4),
+                    rhs_scale=planes1[:, H + cols.start : H + cols.stop],
+                    start=True,
+                    stop=True,
+                )
+
+        h = [keep.tile([P, S], F32, name="h%d" % t) for t in range(PACK)]
+        h_at = [keep.tile([P, S], F32, name="h_at%d" % t) for t in range(PACK)]
+        st = [keep.tile([P, S], F32, name="st%d" % t) for t in range(PACK)]
+        st_at = [keep.tile([P, S], F32, name="st_at%d" % t) for t in range(PACK)]
+        z_planes = keep.tile([P, PACK, S], BF16, align_bytes=64)
+        z_woven = keep.tile([P, S, PACK], BF16, align_bytes=64)
+        z_codes = keep.tile([P, S], U32, align_bytes=64)
+        z_scale = keep.tile([P, S], U8, align_bytes=64)
+        h2_bank = [psum.tile([P, S], F32, name="h2_bank%d" % t) for t in range(PACK)]
+        ex = [keep.tile([P, S], F32, name="ex%d" % t) for t in range(PACK)]
+
+        def weave(engine, woven, planes, cols):
+            dst = woven[:, cols, :].rearrange("p (c i) t -> p c t i", i=4)
+            src = planes[:, :, cols].rearrange("p t (c i) -> p c t i", i=4)
+            if engine == "vector":
+                nc.vector.tensor_copy(out=dst, in_=src)
+            else:
+                nc.scalar.copy(out=dst, in_=src)
+
+        for t in range(PACK):
+            if t == 0:
+                nc.vector.tensor_scalar(h[t][:], h_bank[t][:], gain[:, t : t + 1], None, ALU.mult)
+            else:
+                nc.scalar.activation(out=h[t][:], in_=h_bank[t][:], func=ACT.Copy, scale=gain[:, t : t + 1])
+            for u, cols in enumerate(halves):
+                gather("vector" if t % 2 == 0 else "scalar", h_at[t][:, cols], h[t][:], entries(n1_list, cols))
+            nc.vector.tensor_tensor(out=st[t][:], in0=h[t][:], in1=h_at[t][:], op=ALU.subtract)
+
+        for u, cols in enumerate(halves):
+            for t in range(PACK):
+                gather("scalar", st_at[t][:, cols], st[t][:], entries(n1_list, cols))
+                nc.vector.scalar_tensor_tensor(
+                    out=z_planes[:, t, cols], in0=st_at[t][:, cols], scalar=-0.5, in1=st[t][:, cols],
+                    op0=ALU.mult, op1=ALU.add,
+                )
+            cut = cols.start + 256
+            if cut > cols.start:
+                weave("vector", z_woven, z_planes, slice(cols.start, cut))
+            if cut < cols.stop:
+                weave("scalar", z_woven, z_planes, slice(cut, cols.stop))
+            nc.vector.quantize_mx(
+                out=z_codes[:, cols].bitcast(FP8X4),
+                scales=z_scale[:, cols],
+                in_=z_woven[:, cols, :].rearrange("p c t -> p (c t)"),
+            )
+            for t in range(PACK):
+                rows = slice(t * P, (t + 1) * P)
+                nc.tensor.matmul_mx(
+                    out=h2_bank[t][:, cols],
+                    lhsT=w_dealt[:, rows].bitcast(FP8X4),
+                    lhsT_scale=w_plane[:, rows],
+                    rhs=z_codes[:, cols].bitcast(FP8X4),
+                    rhs_scale=z_scale[:, cols],
+                    start=True,
+                    stop=True,
+                )
+                nc.scalar.activation(out=ex[t][:, cols], in_=h2_bank[t][:, cols], func=ACT.Exp, scale=0.5)
+
+        ex_n2 = keep.tile([P, PACK, S], F32)
+        ex_n3 = keep.tile([P, PACK, S], F32)
+        pair = keep.tile([P, PACK, S], F32)
+        total = keep.tile([P, PACK, S], F32)
+        root = keep.tile([P, PACK, S], F32)
+        inverse = keep.tile([P, PACK, S], F32)
+        y = keep.tile([P, PACK, S], F32)
+        y_woven = keep.tile([P, S, PACK], BF16, align_bytes=64)
+        y_codes = keep.tile([P, S], U32, align_bytes=64)
+        y_scale = keep.tile([P, S], U8, align_bytes=64)
+        out_rows = out_0.rearrange("(p t) j -> p t j", t=PACK)
+        out_words = as_words(out_1)
+        units = [(u, t, cols) for u, cols in enumerate(halves) for t in range(PACK)]
+
+        def fetch(u, t, cols):
+            gather("scalar" if (u == 1 and t >= 2) else "vector", ex_n2[:, t, cols], ex[t][:], entries(n2_list, cols))
+            gather("vector" if (u == 0 and t == 0) else "scalar", ex_n3[:, t, cols], ex[t][:], entries(n3_list, cols))
+
+        def add_first(u, t, cols):
+            nc.vector.tensor_tensor(out=pair[:, t, cols], in0=ex[t][:, cols], in1=ex_n2[:, t, cols], op=ALU.add)
+
+        def add_second(u, t, cols):
+            nc.vector.tensor_tensor(out=total[:, t, cols], in0=pair[:, t, cols], in1=ex_n3[:, t, cols], op=ALU.add)
+
+        def take_root(u, t, cols):
+            nc.scalar.activation(out=root[:, t, cols], in_=total[:, t, cols], func=ACT.Abs_reciprocal_sqrt, scale=0.5)
+
+        def square(u, t, cols):
+            if True:
+                nc.scalar.activation(out=inverse[:, t, cols], in_=root[:, t, cols], func=ACT.Square)
+            else:
+                nc.vector.tensor_tensor(out=inverse[:, t, cols], in0=ex[t][:, cols], in1=root[:, t, cols], op=ALU.mult)
+
+        def finish(u, t, cols):
+            if True:
+                nc.vector.tensor_tensor(out=y[:, t, cols], in0=ex[t][:, cols], in1=inverse[:, t, cols], op=ALU.mult)
+            else:
+                nc.vector.tensor_tensor(out=y[:, t, cols], in0=root[:, t, cols], in1=inverse[:, t, cols], op=ALU.mult)
+            nc.sync.dma_start(out_rows[:, t, cols], y[:, t, cols])
+            if t == PACK - 1:
+                cut = cols.start + 256
+                if cut > cols.start:
+                    weave("vector", y_woven, y, slice(cols.start, cut))
+                if cut < cols.stop:
+                    weave("scalar", y_woven, y, slice(cut, cols.stop))
+                nc.vector.quantize_mx(
+                    out=y_codes[:, cols].bitcast(FP8X4),
+                    scales=y_scale[:, cols],
+                    in_=y_woven[:, cols, :].rearrange("p c t -> p (c t)"),
+                )
+                nc.sync.dma_start(out_words[:, cols], y_codes[:, cols].bitcast(I32))
+
+        stages = [(3, finish), (2, take_root), (1, add_second), (0, fetch), (2, square), (0, add_first)]
+        for step in range(len(units) + max(lag for lag, stage in stages)):
+            for lag, stage in stages:
+                if 0 <= step - lag < len(units):
+                    stage(*units[step - lag])
+        for q in range(4):
+            queue = nc.scalar if q % 2 == 0 else nc.sync
+            queue.dma_start(out_2[0, 4 * q : 4 * q + 4, :].bitcast(I32), y_scale[32 * q : 32 * q + 4, :].bitcast(I32))

@@ -1,6 +1,7 @@
 from contextlib import ExitStack
 
 import concourse.mybir as mybir
+from concourse.masks import make_identity
 
 K, T, S, N, G, H = 512, 2048, 512, 512, 2048, 512
 FLOPS = 2 * K * H * S + 2 * H * N * S
@@ -77,6 +78,9 @@ def tile_picked_hpqtwiceshare_none_po_kernel(
         gain = keep.tile([P, PACK], F32)
         nc.scalar.activation(out=gain[:], in_=gain_raw[:], func=ACT.Copy, scale=0.0625)
 
+        identity = keep.tile([P, P], F32)
+        make_identity(nc, identity[:])
+
         d_bytes_picked = keep.tile([P, H], U8, align_bytes=64)
         x_bytes_picked = keep.tile([P, S], U8, align_bytes=64)
         nc.vector.tensor_copy(out=d_bytes_picked[:], in_=d_bytes[:].indirect(k1_list[:]))
@@ -112,30 +116,8 @@ def tile_picked_hpqtwiceshare_none_po_kernel(
             in_=w_bytes[:].rearrange("p (m t) -> p t m", t=PACK),
         )
 
-        h_bank = [psum.tile([P, S], F32, name="h_bank%d" % t) for t in range(PACK)]
-        for t in range(PACK):
-            rows = slice(t * P, (t + 1) * P)
-            for cols in halves:
-                nc.tensor.matmul_mx(
-                    out=h_bank[t][:, cols],
-                    lhsT=d_dealt[:, rows].bitcast(FP8X4),
-                    lhsT_scale=planes1[:, rows],
-                    rhs=x_picked[:, cols].bitcast(FP8X4),
-                    rhs_scale=planes1[:, H + cols.start : H + cols.stop],
-                    start=True,
-                    stop=True,
-                )
-
-        h = [keep.tile([P, S], F32, name="h%d" % t) for t in range(PACK)]
-        h_at = [keep.tile([P, S], F32, name="h_at%d" % t) for t in range(PACK)]
-        st = [keep.tile([P, S], F32, name="st%d" % t) for t in range(PACK)]
-        st_at = [keep.tile([P, S], F32, name="st_at%d" % t) for t in range(PACK)]
-        z_planes = keep.tile([P, PACK, S], BF16, align_bytes=64)
-        z_woven = keep.tile([P, S, PACK], BF16, align_bytes=64)
-        z_codes = keep.tile([P, S], U32, align_bytes=64)
-        z_scale = keep.tile([P, S], U8, align_bytes=64)
-        h2_bank = [psum.tile([P, S], F32, name="h2_bank%d" % t) for t in range(PACK)]
-        ex = [keep.tile([P, S], F32, name="ex%d" % t) for t in range(PACK)]
+        def bank(name, number):
+            return psum.tile([P, S], F32, name=name, tag="bank%d" % number)
 
         def weave(engine, woven, planes, cols):
             dst = woven[:, cols, :].rearrange("p (c i) t -> p c t i", i=4)
@@ -145,27 +127,70 @@ def tile_picked_hpqtwiceshare_none_po_kernel(
             else:
                 nc.scalar.copy(out=dst, in_=src)
 
-        for t in range(PACK):
-            if t == 0:
-                nc.vector.tensor_scalar(h[t][:], h_bank[t][:], gain[:, t : t + 1], None, ALU.mult)
-            else:
-                nc.scalar.activation(out=h[t][:], in_=h_bank[t][:], func=ACT.Copy, scale=gain[:, t : t + 1])
+        h = [keep.tile([P, S], F32, name="h%d" % t, tag="h%d" % t) for t in range(PACK)]
+        h_bank = {}
+        for t0 in (0, 2):
             for u, cols in enumerate(halves):
-                gather("vector" if t % 2 == 0 else "scalar", h_at[t][:, cols], h[t][:], entries(n1_list, cols))
+                for t in (t0, t0 + 1):
+                    rows = slice(t * P, (t + 1) * P)
+                    h_bank[u, t] = bank("h_bank%d%d" % (u, t), PACK * u + t)
+                    nc.tensor.matmul_mx(
+                        out=h_bank[u, t][:, :HALF],
+                        lhsT=d_dealt[:, rows].bitcast(FP8X4),
+                        lhsT_scale=planes1[:, rows],
+                        rhs=x_picked[:, cols].bitcast(FP8X4),
+                        rhs_scale=planes1[:, H + cols.start : H + cols.stop],
+                        start=True,
+                        stop=True,
+                    )
+
+        def evacuate(t, u):
+            cols = halves[u]
+            if t == 0:
+                nc.vector.tensor_scalar(h[t][:, cols], h_bank[u, t][:, :HALF], gain[:, t : t + 1], None, ALU.mult)
+            else:
+                nc.scalar.activation(out=h[t][:, cols], in_=h_bank[u, t][:, :HALF], func=ACT.Copy, scale=gain[:, t : t + 1])
+
+        h_at = [keep.tile([P, S], F32, name="h_at%d" % t, tag="h_at%d" % t) for t in range(PACK)]
+        st = [keep.tile([P, S], F32, name="st%d" % t) for t in range(PACK)]
+        z_planes = keep.tile([P, PACK, S], BF16, align_bytes=64)
+        z_woven = keep.tile([P, S, PACK], BF16, align_bytes=64)
+        z_codes = keep.tile([P, S], U32, align_bytes=64)
+        z_scale = keep.tile([P, S], U8, align_bytes=64)
+        ex = keep.tile([P, PACK, S], F32)
+        st_at = {}
+        parts1 = halves
+
+        def first_fetch(t, u):
+            gather("vector" if t % 2 == 0 else "scalar", h_at[t][:, halves[u]], h[t][:], entries(n1_list, halves[u]))
+
+        def subtract(t):
             nc.vector.tensor_tensor(out=st[t][:], in0=h[t][:], in1=h_at[t][:], op=ALU.subtract)
 
-        for u, cols in enumerate(halves):
-            for t in range(PACK):
-                gather("scalar", st_at[t][:, cols], st[t][:], entries(n1_list, cols))
-                nc.vector.scalar_tensor_tensor(
-                    out=z_planes[:, t, cols], in0=st_at[t][:, cols], scalar=-0.5, in1=st[t][:, cols],
-                    op0=ALU.mult, op1=ALU.add,
-                )
-            cut = cols.start + 256
+        def second_fetch(t, u):
+            cols = parts1[u]
+            if t % 2 == 0:
+                both = keep.tile([P, 2, cols.stop - cols.start], F32, name="st_at%d%d" % (u, t), tag=("st_at%d" % t if u == 0 else "h_at3" if t == 0 else "h3"))
+                st_at[u, t], st_at[u, t + 1] = both[:, 0, :], both[:, 1, :]
+            gather("vector" if (u == 0 and t == 3) else "scalar", st_at[u, t], st[t][:], entries(n1_list, cols))
+
+        def combine(t, u):
+            cols = parts1[u]
+            nc.vector.scalar_tensor_tensor(
+                out=z_planes[:, t, cols], in0=st_at[u, t], scalar=-0.5, in1=st[t][:, cols], op0=ALU.mult, op1=ALU.add
+            )
+
+        def weave_z(u):
+            cols = parts1[u]
+            cut = cols.start + (256 if u == 0 else 160)
             if cut > cols.start:
                 weave("vector", z_woven, z_planes, slice(cols.start, cut))
             if cut < cols.stop:
                 weave("scalar", z_woven, z_planes, slice(cut, cols.stop))
+
+        def second_product(u):
+            cols = parts1[u]
+            width = cols.stop - cols.start
             nc.vector.quantize_mx(
                 out=z_codes[:, cols].bitcast(FP8X4),
                 scales=z_scale[:, cols],
@@ -173,8 +198,9 @@ def tile_picked_hpqtwiceshare_none_po_kernel(
             )
             for t in range(PACK):
                 rows = slice(t * P, (t + 1) * P)
+                h2_bank = bank("h2_bank%d%d" % (u, t), PACK * (u % 2) + t)
                 nc.tensor.matmul_mx(
-                    out=h2_bank[t][:, cols],
+                    out=h2_bank[:, :width],
                     lhsT=w_dealt[:, rows].bitcast(FP8X4),
                     lhsT_scale=w_plane[:, rows],
                     rhs=z_codes[:, cols].bitcast(FP8X4),
@@ -182,10 +208,25 @@ def tile_picked_hpqtwiceshare_none_po_kernel(
                     start=True,
                     stop=True,
                 )
-                nc.scalar.activation(out=ex[t][:, cols], in_=h2_bank[t][:, cols], func=ACT.Exp, scale=0.5)
+                nc.scalar.activation(out=ex[:, t, cols], in_=h2_bank[:, :width], func=ACT.Exp, scale=0.5)
 
-        ex_n2 = keep.tile([P, PACK, S], F32)
-        ex_n3 = keep.tile([P, PACK, S], F32)
+        for t in range(PACK):
+            evacuate(t, 0)
+            evacuate(t, 1)
+            first_fetch(t, 0)
+            first_fetch(t, 1)
+            if t > 0:
+                subtract(t - 1)
+        subtract(PACK - 1)
+        for u in range(len(parts1)):
+            for t in range(PACK):
+                second_fetch(t, u)
+                combine(t, u)
+            weave_z(u)
+            second_product(u)
+
+        ex_n2 = {}
+        ex_n3 = {}
         pair = keep.tile([P, PACK, S], F32)
         total = keep.tile([P, PACK, S], F32)
         root = keep.tile([P, PACK, S], F32)
@@ -196,35 +237,72 @@ def tile_picked_hpqtwiceshare_none_po_kernel(
         y_scale = keep.tile([P, S], U8, align_bytes=64)
         out_rows = out_0.rearrange("(p t) j -> p t j", t=PACK)
         out_words = as_words(out_1)
-        units = [(u, t, cols) for u, cols in enumerate(halves) for t in range(PACK)]
+        units = [(u, t, cols) for u, cols in enumerate([slice(0, 256), slice(256, 384), slice(384, 512)]) for t in range(PACK)]
+        sums = {}
+        back = {}
+
+        def on_pe(u, t):
+            return True
 
         def fetch(u, t, cols):
-            gather("scalar" if (u == 1 and t >= 2) else "vector", ex_n2[:, t, cols], ex[t][:], entries(n2_list, cols))
-            gather("vector" if (u == 0 and t == 0) else "scalar", ex_n3[:, t, cols], ex[t][:], entries(n3_list, cols))
+            width = cols.stop - cols.start
+            ex_n2[u, t] = keep.tile([P, width], F32, name="ex_n2_%d%d" % (u, t), tag="ex_n2_%d" % t)
+            ex_n3[u, t] = keep.tile([P, width], F32, name="ex_n3_%d%d" % (u, t), tag="ex_n3_%d" % t)
+            gather("vector", ex_n2[u, t][:], ex[:, t, :], entries(n2_list, cols))
+            gather("scalar" if (u == 0 and t > 0) or u == 2 else "vector", ex_n3[u, t][:], ex[:, t, :], entries(n3_list, cols))
 
         def add_first(u, t, cols):
-            nc.vector.tensor_tensor(out=pair[:, t, cols], in0=ex[t][:, cols], in1=ex_n2[:, t, cols], op=ALU.add)
+            if not on_pe(u, t):
+                nc.vector.tensor_tensor(out=pair[:, t, cols], in0=ex[:, t, cols], in1=ex_n2[u, t][:], op=ALU.add)
 
         def add_second(u, t, cols):
-            nc.vector.tensor_tensor(out=total[:, t, cols], in0=pair[:, t, cols], in1=ex_n3[:, t, cols], op=ALU.add)
+            if not on_pe(u, t):
+                nc.vector.tensor_tensor(out=total[:, t, cols], in0=pair[:, t, cols], in1=ex_n3[u, t][:], op=ALU.add)
+                return
+            width = cols.stop - cols.start
+            sums[u, t] = bank("sums%d%d" % (u, t), PACK + t)
+            terms = (ex[:, t, cols], ex_n2[u, t], ex_n3[u, t])
+            for j, term in enumerate(terms):
+                for c in range(0, width, P):
+                    nc.tensor.matmul(
+                        sums[u, t][:, c : c + P], term[:, c : c + P], identity[:],
+                        start=(j == 0 and c == 0), stop=(j == 2 and c == width - P), is_transpose=True,
+                    )
 
         def take_root(u, t, cols):
-            nc.scalar.activation(out=root[:, t, cols], in_=total[:, t, cols], func=ACT.Abs_reciprocal_sqrt, scale=0.5)
+            width = cols.stop - cols.start
+            src = sums[u, t][:, :width] if on_pe(u, t) else total[:, t, cols]
+            nc.scalar.activation(out=root[:, t, cols], in_=src, func=ACT.Abs_reciprocal_sqrt, scale=0.5)
+
+        def turn_back(u, t, cols, src):
+            width = cols.stop - cols.start
+            back[u, t] = bank("back%d%d" % (u, t), t)
+            for c in range(0, width, P):
+                nc.tensor.transpose(back[u, t][:, c : c + P], src[:, t, cols.start + c : cols.start + c + P], identity[:])
 
         def square(u, t, cols):
+            width = cols.stop - cols.start
             if True:
                 nc.scalar.activation(out=inverse[:, t, cols], in_=root[:, t, cols], func=ACT.Square)
+                if on_pe(u, t):
+                    turn_back(u, t, cols, inverse)
             else:
-                nc.vector.tensor_tensor(out=inverse[:, t, cols], in0=ex[t][:, cols], in1=root[:, t, cols], op=ALU.mult)
+                if on_pe(u, t):
+                    turn_back(u, t, cols, root)
+                src = back[u, t][:, :width] if on_pe(u, t) else root[:, t, cols]
+                nc.vector.tensor_tensor(out=inverse[:, t, cols], in0=ex[:, t, cols], in1=src, op=ALU.mult)
 
         def finish(u, t, cols):
+            width = cols.stop - cols.start
             if True:
-                nc.vector.tensor_tensor(out=y[:, t, cols], in0=ex[t][:, cols], in1=inverse[:, t, cols], op=ALU.mult)
+                src = back[u, t][:, :width] if on_pe(u, t) else inverse[:, t, cols]
+                nc.vector.tensor_tensor(out=y[:, t, cols], in0=ex[:, t, cols], in1=src, op=ALU.mult)
             else:
-                nc.vector.tensor_tensor(out=y[:, t, cols], in0=root[:, t, cols], in1=inverse[:, t, cols], op=ALU.mult)
-            nc.sync.dma_start(out_rows[:, t, cols], y[:, t, cols])
+                src = back[u, t][:, :width] if on_pe(u, t) else root[:, t, cols]
+                nc.vector.tensor_tensor(out=y[:, t, cols], in0=inverse[:, t, cols], in1=src, op=ALU.mult)
             if t == PACK - 1:
-                cut = cols.start + 256
+                nc.sync.dma_start(out_rows[:, :, cols], y[:, :, cols])
+                cut = cols.start + cols.stop - cols.start
                 if cut > cols.start:
                     weave("vector", y_woven, y, slice(cols.start, cut))
                 if cut < cols.stop:
@@ -236,7 +314,7 @@ def tile_picked_hpqtwiceshare_none_po_kernel(
                 )
                 nc.sync.dma_start(out_words[:, cols], y_codes[:, cols].bitcast(I32))
 
-        stages = [(3, finish), (2, take_root), (1, add_second), (0, fetch), (2, square), (0, add_first)]
+        stages = [(4, finish), (0, fetch), (0, add_first), (0, add_second), (0, take_root), (0, square)]
         for step in range(len(units) + max(lag for lag, stage in stages)):
             for lag, stage in stages:
                 if 0 <= step - lag < len(units):

@@ -50,27 +50,25 @@ def tile_picked_hpqtwiceshare_none_po_kernel(
         n3_list = keep.tile([P, S // 16], U16)
         d_bytes = keep.tile([P, G], U8, align_bytes=64)
         x_bytes = keep.tile([P, T], U8, align_bytes=64)
+        planes1 = keep.tile([P, H + S], U8, align_bytes=64)
+        w_bytes = keep.tile([P, N], U8, align_bytes=64)
+        for plane in (planes1, w_bytes):
+            nc.gpsimd.memset(plane[:].bitcast(I32), 0)
         nc.sync.dma_start(k1_list[:], k1)
         nc.sync.dma_start(d_bytes[:].bitcast(I32), d_scales[0].bitcast(I32).unsqueeze(1).broadcast_to([16, 8, G // 4]))
         nc.sync.dma_start(offs_list[:], offs)
         nc.sync.dma_start(x_bytes[:].bitcast(I32), x_scales[0].bitcast(I32).unsqueeze(1).broadcast_to([16, 8, T // 4]))
         nc.sync.dma_start(n1_list[:], n1)
-        nc.sync.dma_start(n2_list[:], n2)
 
         d_table = keep.tile([P, G], U32, align_bytes=64)
         x_table = keep.tile([P, T], U32, align_bytes=64, tag="x_table")
-        w_table = keep.tile([P, N], U32, align_bytes=64)
         nc.sync.dma_start(d_table[:].bitcast(I32), as_words(d_words))
         nc.sync.dma_start(x_table[:].bitcast(I32), as_words(x_words))
-        nc.sync.dma_start(w_table[:].bitcast(I32), as_words(w1_words))
+        nc.sync.dma_start(n2_list[:], n2)
         nc.sync.dma_start(n3_list[:], n3)
 
         gain_raw = keep.tile([P, PACK], F32)
         nc.gpsimd.dma_start(gain_raw[:], gn.rearrange("(p t) o -> p (t o)", t=PACK))
-        w_bytes = keep.tile([P, N], U8, align_bytes=64)
-        nc.gpsimd.memset(w_bytes[:].bitcast(I32), 0)
-        planes1 = keep.tile([P, H + S], U8, align_bytes=64)
-        nc.gpsimd.memset(planes1[:].bitcast(I32), 0)
         for q in range(4):
             nc.gpsimd.dma_start(
                 w_bytes[32 * q : 32 * q + 4, :].bitcast(I32), w1_scales[0, 4 * q : 4 * q + 4, :].bitcast(I32)
@@ -82,17 +80,19 @@ def tile_picked_hpqtwiceshare_none_po_kernel(
         make_identity(nc, identity[:])
 
         d_bytes_picked = keep.tile([P, H], U8, align_bytes=64)
-        x_bytes_picked = keep.tile([P, S], U8, align_bytes=64)
+        x_bytes_picked = keep.tile([P, S], U8, align_bytes=64, tag="x_bytes_picked")
         nc.vector.tensor_copy(out=d_bytes_picked[:], in_=d_bytes[:].indirect(k1_list[:]))
+        nc.vector.tensor_copy(out=x_bytes_picked[:], in_=x_bytes[:].indirect(offs_list[:]))
         joined = keep.tile([P, H + S], U8, align_bytes=64)
         nc.vector.tensor_copy(
             out=joined[:, :H].rearrange("p (t m) -> p t m", t=PACK),
             in_=d_bytes_picked[:].rearrange("p (m t) -> p t m", t=PACK),
         )
-        nc.vector.tensor_copy(out=x_bytes_picked[:], in_=x_bytes[:].indirect(offs_list[:]))
         nc.vector.tensor_copy(out=joined[:, H:].bitcast(I32), in_=x_bytes_picked[:].bitcast(I32))
         for c in range(4):
-            nc.scalar.dma_start(planes1[c:P:32, :].bitcast(I32), joined[8 * c : P : 32, :].bitcast(I32))
+            nc.sync.dma_start(planes1[c:P:32, :].bitcast(I32), joined[8 * c : P : 32, :].bitcast(I32))
+        w_table = keep.tile([P, N], U32, align_bytes=64, tag="x_bytes_picked")
+        nc.sync.dma_start(w_table[:].bitcast(I32), as_words(w1_words))
 
         d_picked = keep.tile([P, H], U32, align_bytes=64)
         d_dealt = keep.tile([P, H], U32, align_bytes=64)
@@ -159,7 +159,7 @@ def tile_picked_hpqtwiceshare_none_po_kernel(
         z_scale = keep.tile([P, S], U8, align_bytes=64)
         ex = keep.tile([P, PACK, S], F32)
         st_at = {}
-        parts1 = halves
+        parts1 = [slice(0, 256), slice(256, 384), slice(384, 512)]
 
         def first_fetch(t, u):
             gather("vector" if t % 2 == 0 else "scalar", h_at[t][:, halves[u]], h[t][:], entries(n1_list, halves[u]))
@@ -170,9 +170,9 @@ def tile_picked_hpqtwiceshare_none_po_kernel(
         def second_fetch(t, u):
             cols = parts1[u]
             if t % 2 == 0:
-                both = keep.tile([P, 2, cols.stop - cols.start], F32, name="st_at%d%d" % (u, t), tag=("st_at%d" % t if u == 0 else "h_at3" if t == 0 else "h3"))
+                both = keep.tile([P, 2, cols.stop - cols.start], F32, name="st_at%d%d" % (u, t), tag=("st_at%d" % t if u != 1 else "h_at3" if t == 0 else "h3"))
                 st_at[u, t], st_at[u, t + 1] = both[:, 0, :], both[:, 1, :]
-            gather("vector" if (u == 0 and t == 3) else "scalar", st_at[u, t], st[t][:], entries(n1_list, cols))
+            gather("scalar", st_at[u, t], st[t][:], entries(n1_list, cols))
 
         def combine(t, u):
             cols = parts1[u]
@@ -182,7 +182,7 @@ def tile_picked_hpqtwiceshare_none_po_kernel(
 
         def weave_z(u):
             cols = parts1[u]
-            cut = cols.start + (256 if u == 0 else 160)
+            cut = cols.start + cols.stop - cols.start
             if cut > cols.start:
                 weave("vector", z_woven, z_planes, slice(cols.start, cut))
             if cut < cols.stop:
@@ -260,7 +260,7 @@ def tile_picked_hpqtwiceshare_none_po_kernel(
                 nc.vector.tensor_tensor(out=total[:, t, cols], in0=pair[:, t, cols], in1=ex_n3[u, t][:], op=ALU.add)
                 return
             width = cols.stop - cols.start
-            sums[u, t] = bank("sums%d%d" % (u, t), PACK + t)
+            sums[u, t] = bank("sums%d%d" % (u, t), t)
             terms = (ex[:, t, cols], ex_n2[u, t], ex_n3[u, t])
             for j, term in enumerate(terms):
                 for c in range(0, width, P):
@@ -276,7 +276,7 @@ def tile_picked_hpqtwiceshare_none_po_kernel(
 
         def turn_back(u, t, cols, src):
             width = cols.stop - cols.start
-            back[u, t] = bank("back%d%d" % (u, t), t)
+            back[u, t] = bank("back%d%d" % (u, t), PACK + t)
             for c in range(0, width, P):
                 nc.tensor.transpose(back[u, t][:, c : c + P], src[:, t, cols.start + c : cols.start + c + P], identity[:])
 

@@ -51,33 +51,25 @@ def tile_picked_hpqtwiceshare_none_po_kernel(
         d_bytes = keep.tile([P, G], U8, align_bytes=64)
         x_bytes = keep.tile([P, T], U8, align_bytes=64)
         planes1 = keep.tile([P, H + S], U8, align_bytes=64)
-        w_bytes = keep.tile([P, N], U8, align_bytes=64)
-        for plane in (planes1, w_bytes):
-            nc.gpsimd.memset(plane[:].bitcast(I32), 0)
+        nc.gpsimd.memset(planes1[:].bitcast(I32), 0)
+        identity = keep.tile([P, P], F32)
+        make_identity(nc, identity[:])
         nc.sync.dma_start(k1_list[:], k1)
         nc.sync.dma_start(d_bytes[:].bitcast(I32), d_scales[0].bitcast(I32).unsqueeze(1).broadcast_to([16, 8, G // 4]))
         nc.sync.dma_start(offs_list[:], offs)
         nc.sync.dma_start(x_bytes[:].bitcast(I32), x_scales[0].bitcast(I32).unsqueeze(1).broadcast_to([16, 8, T // 4]))
-        nc.sync.dma_start(n1_list[:], n1)
 
-        d_table = keep.tile([P, G], U32, align_bytes=64)
+        d_table = keep.tile([P, G], U32, align_bytes=64, tag="d_table")
         x_table = keep.tile([P, T], U32, align_bytes=64, tag="x_table")
-        nc.sync.dma_start(d_table[:].bitcast(I32), as_words(d_words))
-        nc.sync.dma_start(x_table[:].bitcast(I32), as_words(x_words))
-        nc.sync.dma_start(n2_list[:], n2)
-        nc.sync.dma_start(n3_list[:], n3)
-
         gain_raw = keep.tile([P, PACK], F32)
-        nc.gpsimd.dma_start(gain_raw[:], gn.rearrange("(p t) o -> p (t o)", t=PACK))
-        for q in range(4):
-            nc.gpsimd.dma_start(
-                w_bytes[32 * q : 32 * q + 4, :].bitcast(I32), w1_scales[0, 4 * q : 4 * q + 4, :].bitcast(I32)
-            )
+        nc.sync.dma_start(d_table[:].bitcast(I32), as_words(d_words))
+        nc.sync.dma_start(n1_list[:], n1)
+        nc.sync.dma_start(n2_list[:], n2)
+        nc.sync.dma_start(gain_raw[:], gn.rearrange("(p t) o -> p (t o)", t=PACK))
+        nc.sync.dma_start(x_table[:].bitcast(I32), as_words(x_words))
+        nc.sync.dma_start(n3_list[:], n3)
         gain = keep.tile([P, PACK], F32)
         nc.scalar.activation(out=gain[:], in_=gain_raw[:], func=ACT.Copy, scale=0.0625)
-
-        identity = keep.tile([P, P], F32)
-        make_identity(nc, identity[:])
 
         d_bytes_picked = keep.tile([P, H], U8, align_bytes=64)
         x_bytes_picked = keep.tile([P, S], U8, align_bytes=64, tag="x_bytes_picked")
@@ -105,6 +97,10 @@ def tile_picked_hpqtwiceshare_none_po_kernel(
         for cols in halves:
             nc.vector.tensor_copy(out=x_picked[:, cols], in_=x_table[:].indirect(entries(offs_list, cols)))
 
+        w_bytes = keep.tile([P, N], U8, align_bytes=64, tag="d_table")
+        for q in range(4):
+            rows = w1_scales[0, 4 * q : 4 * q + 4, :].bitcast(I32)
+            nc.sync.dma_start(w_bytes[32 * q : 32 * q + 32, :].bitcast(I32), rows.unsqueeze(0).broadcast_to([8, 4, N // 4]))
         w_dealt = keep.tile([P, N], U32, align_bytes=64)
         nc.scalar.copy(
             out=w_dealt[:].rearrange("p (t c i) -> p c t i", t=PACK, i=4),
@@ -242,7 +238,7 @@ def tile_picked_hpqtwiceshare_none_po_kernel(
         back = {}
 
         def on_pe(u, t):
-            return True
+            return not (u == 2 and t >= 2)
 
         def fetch(u, t, cols):
             width = cols.stop - cols.start
@@ -282,7 +278,7 @@ def tile_picked_hpqtwiceshare_none_po_kernel(
 
         def square(u, t, cols):
             width = cols.stop - cols.start
-            if True:
+            if not (u == 2 and t >= 2):
                 nc.scalar.activation(out=inverse[:, t, cols], in_=root[:, t, cols], func=ACT.Square)
                 if on_pe(u, t):
                     turn_back(u, t, cols, inverse)
@@ -294,7 +290,7 @@ def tile_picked_hpqtwiceshare_none_po_kernel(
 
         def finish(u, t, cols):
             width = cols.stop - cols.start
-            if True:
+            if not (u == 2 and t >= 2):
                 src = back[u, t][:, :width] if on_pe(u, t) else inverse[:, t, cols]
                 nc.vector.tensor_tensor(out=y[:, t, cols], in0=ex[:, t, cols], in1=src, op=ALU.mult)
             else:

@@ -18,187 +18,199 @@ ACT = mybir.ActivationFunctionType
 
 P = 128
 PACK = 4
+GROUP = 16
+QUADRANT = 32
+BLOCKS = K // 32
+BLOCK_PARTITIONS = P // BLOCKS
+LINE = 4
 HALF = S // 2
+HALVES = [slice(0, HALF), slice(HALF, S)]
+PARTS = [slice(0, 256), slice(256, 384), slice(384, 512)]
+LAST_PART = len(PARTS) - 1
 
 
 def tile_picked_hpqtwiceshare_none_po_kernel(
     tc, x_words, x_scales, d_words, d_scales, gn, w1_words, w1_scales, offs, k1, n1, n2, n3, out_0, out_1, out_2
 ):
     nc = tc.nc
-    halves = [slice(0, HALF), slice(HALF, S)]
 
-    def entries(lst, cols):
-        return lst[:, cols.start // 16 : cols.stop // 16]
+    def entries(offsets, cols):
+        return offsets[:, cols.start // GROUP : cols.stop // GROUP]
 
-    def gather(engine, out, window, offsets):
-        if engine == "vector":
-            nc.vector.tensor_copy(out=out, in_=window.indirect(offsets))
-        else:
-            nc.scalar.activation(out=out, in_=window.indirect(offsets), func=ACT.Copy)
+    def vector_gather(out, window, offsets):
+        nc.vector.tensor_copy(out=out, in_=window.indirect(offsets))
+
+    def scalar_gather(out, window, offsets):
+        nc.scalar.activation(out=out, in_=window.indirect(offsets), func=ACT.Copy)
 
     def as_words(packed):
         return packed[0].rearrange("p n t -> p (n t)").bitcast(I32)
+
+    def spread_rows(scales):
+        scale_rows = scales[0].bitcast(I32)
+        return scale_rows.unsqueeze(1).broadcast_to([BLOCKS, BLOCK_PARTITIONS, scale_rows.shape[1]])
+
+    def dealt_words(dealt):
+        return dealt.rearrange("p (t c i) -> p c t i", t=PACK, i=LINE)
+
+    def plain_words(plain):
+        return plain.rearrange("p (c i t) -> p c t i", t=PACK, i=LINE)
+
+    def deal_bytes(dealt, plain):
+        nc.vector.tensor_copy(
+            out=dealt.rearrange("p (t m) -> p t m", t=PACK), in_=plain.rearrange("p (m t) -> p t m", t=PACK)
+        )
+
+    def weave_and_quantize(tiles, woven, codes, scales, cols):
+        nc.vector.tensor_copy(
+            out=woven[:, cols, :].rearrange("p (c i) t -> p c t i", i=LINE),
+            in_=tiles[:, :, cols].rearrange("p t (c i) -> p c t i", i=LINE),
+        )
+        nc.vector.quantize_mx(
+            out=codes[:, cols].bitcast(FP8X4),
+            scales=scales[:, cols],
+            in_=woven[:, cols, :].rearrange("p c t -> p (c t)"),
+        )
 
     with ExitStack() as ctx:
         keep = ctx.enter_context(tc.tile_pool(name="keep", bufs=1))
         psum = ctx.enter_context(tc.psum_pool(name="psum", bufs=1))
 
-        k1_list = keep.tile([P, H // 16], U16)
-        offs_list = keep.tile([P, S // 16], U16)
-        n1_list = keep.tile([P, S // 16], U16)
-        n2_list = keep.tile([P, S // 16], U16)
-        n3_list = keep.tile([P, S // 16], U16)
+        def bank(name, number):
+            return psum.tile([P, S], F32, name=name, tag="bank%d" % number)
+
+        k1_list = keep.tile([P, H // GROUP], U16)
+        offs_list = keep.tile([P, S // GROUP], U16)
+        n1_list = keep.tile([P, S // GROUP], U16)
+        n2_list = keep.tile([P, S // GROUP], U16)
+        n3_list = keep.tile([P, S // GROUP], U16)
         d_bytes = keep.tile([P, G], U8, align_bytes=64)
         x_bytes = keep.tile([P, T], U8, align_bytes=64)
-        planes1 = keep.tile([P, H + S], U8, align_bytes=64)
-        nc.gpsimd.memset(planes1[:].bitcast(I32), 0)
+        first_scales = keep.tile([P, H + S], U8, align_bytes=64)
+        nc.gpsimd.memset(first_scales[:].bitcast(I32), 0)
         identity = keep.tile([P, P], F32)
         make_identity(nc, identity[:])
         nc.sync.dma_start(k1_list[:], k1)
-        nc.sync.dma_start(d_bytes[:].bitcast(I32), d_scales[0].bitcast(I32).unsqueeze(1).broadcast_to([16, 8, G // 4]))
+        nc.sync.dma_start(d_bytes[:].bitcast(I32), spread_rows(d_scales))
         nc.sync.dma_start(offs_list[:], offs)
-        nc.sync.dma_start(x_bytes[:].bitcast(I32), x_scales[0].bitcast(I32).unsqueeze(1).broadcast_to([16, 8, T // 4]))
+        nc.sync.dma_start(x_bytes[:].bitcast(I32), spread_rows(x_scales))
 
         d_table = keep.tile([P, G], U32, align_bytes=64, tag="d_table")
         x_table = keep.tile([P, T], U32, align_bytes=64, tag="x_table")
-        gain_raw = keep.tile([P, PACK], F32)
+        gn_rows = keep.tile([P, PACK], F32)
         nc.sync.dma_start(d_table[:].bitcast(I32), as_words(d_words))
         nc.sync.dma_start(n1_list[:], n1)
         nc.sync.dma_start(n2_list[:], n2)
-        nc.sync.dma_start(gain_raw[:], gn.rearrange("(p t) o -> p (t o)", t=PACK))
+        nc.sync.dma_start(gn_rows[:], gn.rearrange("(p t) o -> p (t o)", t=PACK))
         nc.sync.dma_start(x_table[:].bitcast(I32), as_words(x_words))
         nc.sync.dma_start(n3_list[:], n3)
         gain = keep.tile([P, PACK], F32)
-        nc.scalar.activation(out=gain[:], in_=gain_raw[:], func=ACT.Copy, scale=0.0625)
+        nc.scalar.activation(out=gain[:], in_=gn_rows[:], func=ACT.Copy, scale=0.0625)
 
         d_bytes_picked = keep.tile([P, H], U8, align_bytes=64)
         x_bytes_picked = keep.tile([P, S], U8, align_bytes=64, tag="x_bytes_picked")
-        nc.vector.tensor_copy(out=d_bytes_picked[:], in_=d_bytes[:].indirect(k1_list[:]))
-        nc.vector.tensor_copy(out=x_bytes_picked[:], in_=x_bytes[:].indirect(offs_list[:]))
+        vector_gather(d_bytes_picked[:], d_bytes[:], k1_list[:])
+        vector_gather(x_bytes_picked[:], x_bytes[:], offs_list[:])
         joined = keep.tile([P, H + S], U8, align_bytes=64)
-        nc.vector.tensor_copy(
-            out=joined[:, :H].rearrange("p (t m) -> p t m", t=PACK),
-            in_=d_bytes_picked[:].rearrange("p (m t) -> p t m", t=PACK),
-        )
+        deal_bytes(joined[:, :H], d_bytes_picked[:])
         nc.vector.tensor_copy(out=joined[:, H:].bitcast(I32), in_=x_bytes_picked[:].bitcast(I32))
-        for c in range(4):
-            nc.sync.dma_start(planes1[c:P:32, :].bitcast(I32), joined[8 * c : P : 32, :].bitcast(I32))
+        for r in range(PACK):
+            nc.sync.dma_start(
+                first_scales[r:P:QUADRANT, :].bitcast(I32),
+                joined[BLOCK_PARTITIONS * r : P : QUADRANT, :].bitcast(I32),
+            )
         w_table = keep.tile([P, N], U32, align_bytes=64, tag="x_bytes_picked")
         nc.sync.dma_start(w_table[:].bitcast(I32), as_words(w1_words))
 
         d_picked = keep.tile([P, H], U32, align_bytes=64)
         d_dealt = keep.tile([P, H], U32, align_bytes=64)
         x_picked = keep.tile([P, S], U32, align_bytes=64)
-        nc.vector.tensor_copy(out=d_picked[:], in_=d_table[:].indirect(k1_list[:]))
-        nc.vector.tensor_copy(
-            out=d_dealt[:].rearrange("p (t c i) -> p c t i", t=PACK, i=4),
-            in_=d_picked[:].rearrange("p (c i t) -> p c t i", t=PACK, i=4),
-        )
-        for cols in halves:
-            nc.vector.tensor_copy(out=x_picked[:, cols], in_=x_table[:].indirect(entries(offs_list, cols)))
+        vector_gather(d_picked[:], d_table[:], k1_list[:])
+        nc.vector.tensor_copy(out=dealt_words(d_dealt[:]), in_=plain_words(d_picked[:]))
+        for cols in HALVES:
+            vector_gather(x_picked[:, cols], x_table[:], entries(offs_list, cols))
 
         w_bytes = keep.tile([P, N], U8, align_bytes=64, tag="d_table")
-        for q in range(4):
-            rows = w1_scales[0, 4 * q : 4 * q + 4, :].bitcast(I32)
-            nc.sync.dma_start(w_bytes[32 * q : 32 * q + 32, :].bitcast(I32), rows.unsqueeze(0).broadcast_to([8, 4, N // 4]))
+        for q in range(P // QUADRANT):
+            scale_rows = w1_scales[0, PACK * q : PACK * (q + 1), :].bitcast(I32)
+            nc.sync.dma_start(
+                w_bytes[QUADRANT * q : QUADRANT * (q + 1), :].bitcast(I32),
+                scale_rows.unsqueeze(0).broadcast_to([QUADRANT // PACK, PACK, scale_rows.shape[1]]),
+            )
         w_dealt = keep.tile([P, N], U32, align_bytes=64)
-        nc.scalar.copy(
-            out=w_dealt[:].rearrange("p (t c i) -> p c t i", t=PACK, i=4),
-            in_=w_table[:].rearrange("p (c i t) -> p c t i", t=PACK, i=4),
-        )
-        w_plane = keep.tile([P, N], U8, align_bytes=64, tag="x_table")
-        nc.vector.tensor_copy(
-            out=w_plane[:].rearrange("p (t m) -> p t m", t=PACK),
-            in_=w_bytes[:].rearrange("p (m t) -> p t m", t=PACK),
-        )
+        nc.scalar.copy(out=dealt_words(w_dealt[:]), in_=plain_words(w_table[:]))
+        w_scale = keep.tile([P, N], U8, align_bytes=64, tag="x_table")
+        deal_bytes(w_scale[:], w_bytes[:])
 
-        def bank(name, number):
-            return psum.tile([P, S], F32, name=name, tag="bank%d" % number)
-
-        def weave(engine, woven, planes, cols):
-            dst = woven[:, cols, :].rearrange("p (c i) t -> p c t i", i=4)
-            src = planes[:, :, cols].rearrange("p t (c i) -> p c t i", i=4)
-            if engine == "vector":
-                nc.vector.tensor_copy(out=dst, in_=src)
-            else:
-                nc.scalar.copy(out=dst, in_=src)
-
-        h = [keep.tile([P, S], F32, name="h%d" % t, tag="h%d" % t) for t in range(PACK)]
+        h = [keep.tile([P, 2 * S], F32, name="h%d" % t, tag="h%d" % t) for t in range(PACK)]
+        for t in range(PACK):
+            clearing = nc.vector if t % 2 == 0 else nc.gpsimd
+            clearing.memset(h[t][:, S:], 0.0)
         h_bank = {}
-        for t0 in (0, 2):
-            for u, cols in enumerate(halves):
-                for t in (t0, t0 + 1):
+        for pair_of_tiles in ((0, 1), (2, 3)):
+            for half, cols in enumerate(HALVES):
+                for t in pair_of_tiles:
                     rows = slice(t * P, (t + 1) * P)
-                    h_bank[u, t] = bank("h_bank%d%d" % (u, t), PACK * u + t)
+                    h_bank[half, t] = bank("h_bank%d%d" % (half, t), PACK * half + t)
                     nc.tensor.matmul_mx(
-                        out=h_bank[u, t][:, :HALF],
+                        out=h_bank[half, t][:, :HALF],
                         lhsT=d_dealt[:, rows].bitcast(FP8X4),
-                        lhsT_scale=planes1[:, rows],
+                        lhsT_scale=first_scales[:, rows],
                         rhs=x_picked[:, cols].bitcast(FP8X4),
-                        rhs_scale=planes1[:, H + cols.start : H + cols.stop],
+                        rhs_scale=first_scales[:, H + cols.start : H + cols.stop],
                         start=True,
                         stop=True,
                     )
 
-        def evacuate(t, u):
-            cols = halves[u]
-            if t == 0:
-                nc.vector.tensor_scalar(h[t][:, cols], h_bank[u, t][:, :HALF], gain[:, t : t + 1], None, ALU.mult)
-            else:
-                nc.scalar.activation(out=h[t][:, cols], in_=h_bank[u, t][:, :HALF], func=ACT.Copy, scale=gain[:, t : t + 1])
-
         h_at = [keep.tile([P, S], F32, name="h_at%d" % t, tag="h_at%d" % t) for t in range(PACK)]
         st = [keep.tile([P, S], F32, name="st%d" % t) for t in range(PACK)]
-        z_planes = keep.tile([P, PACK, S], BF16, align_bytes=64)
+        z_tiles = keep.tile([P, PACK, S], BF16, align_bytes=64)
         z_woven = keep.tile([P, S, PACK], BF16, align_bytes=64)
         z_codes = keep.tile([P, S], U32, align_bytes=64)
         z_scale = keep.tile([P, S], U8, align_bytes=64)
         ex = keep.tile([P, PACK, S], F32)
-        st_at = {}
-        parts1 = [slice(0, 256), slice(256, 384), slice(384, 512)]
-
-        def first_fetch(t, u):
-            gather("vector" if t % 2 == 0 else "scalar", h_at[t][:, halves[u]], h[t][:], entries(n1_list, halves[u]))
 
         def subtract(t):
-            nc.vector.tensor_tensor(out=st[t][:], in0=h[t][:], in1=h_at[t][:], op=ALU.subtract)
+            nc.vector.tensor_tensor(out=st[t][:], in0=h[t][:, :S], in1=h_at[t][:], op=ALU.subtract)
 
-        def second_fetch(t, u):
-            cols = parts1[u]
-            if t % 2 == 0:
-                both = keep.tile([P, 2, cols.stop - cols.start], F32, name="st_at%d%d" % (u, t), tag=("st_at%d" % t if u != 1 else "h_at3" if t == 0 else "h3"))
-                st_at[u, t], st_at[u, t + 1] = both[:, 0, :], both[:, 1, :]
-            gather("scalar", st_at[u, t], st[t][:], entries(n1_list, cols))
+        for t in range(PACK):
+            for half, cols in enumerate(HALVES):
+                product = h_bank[half, t][:, :HALF]
+                if t == 0:
+                    nc.vector.tensor_scalar(h[t][:, cols], product, gain[:, t : t + 1], None, ALU.mult)
+                else:
+                    nc.scalar.activation(out=h[t][:, cols], in_=product, func=ACT.Copy, scale=gain[:, t : t + 1])
+            gather = vector_gather if t % 2 == 0 else scalar_gather
+            gather(h_at[t][:], h[t][:], n1_list[:])
+            if t > 0:
+                subtract(t - 1)
+        subtract(PACK - 1)
 
-        def combine(t, u):
-            cols = parts1[u]
-            nc.vector.scalar_tensor_tensor(
-                out=z_planes[:, t, cols], in0=st_at[u, t], scalar=-0.5, in1=st[t][:, cols], op0=ALU.mult, op1=ALU.add
-            )
-
-        def weave_z(u):
-            cols = parts1[u]
-            cut = cols.start + cols.stop - cols.start
-            if cut > cols.start:
-                weave("vector", z_woven, z_planes, slice(cols.start, cut))
-            if cut < cols.stop:
-                weave("scalar", z_woven, z_planes, slice(cut, cols.stop))
-
-        def second_product(u):
-            cols = parts1[u]
+        st_at_buffers = [("st_at0", "st_at2"), ("h_at3", "h3"), ("st_at0", "st_at2")]
+        for part, cols in enumerate(PARTS):
             width = cols.stop - cols.start
-            nc.vector.quantize_mx(
-                out=z_codes[:, cols].bitcast(FP8X4),
-                scales=z_scale[:, cols],
-                in_=z_woven[:, cols, :].rearrange("p c t -> p (c t)"),
-            )
+            for t in range(PACK):
+                if t % 2 == 0:
+                    st_at = keep.tile(
+                        [P, 2, width], F32, name="st_at%d%d" % (part, t), tag=st_at_buffers[part][t // 2]
+                    )
+                scalar_gather(st_at[:, t % 2, :], st[t][:], entries(n1_list, cols))
+                nc.vector.scalar_tensor_tensor(
+                    out=z_tiles[:, t, cols],
+                    in0=st_at[:, t % 2, :],
+                    scalar=-0.5,
+                    in1=st[t][:, cols],
+                    op0=ALU.mult,
+                    op1=ALU.add,
+                )
+            weave_and_quantize(z_tiles, z_woven, z_codes, z_scale, cols)
             for t in range(PACK):
                 rows = slice(t * P, (t + 1) * P)
-                h2_bank = bank("h2_bank%d%d" % (u, t), PACK * (u % 2) + t)
+                h2_bank = bank("h2_bank%d%d" % (part, t), PACK * (part % 2) + t)
                 nc.tensor.matmul_mx(
                     out=h2_bank[:, :width],
                     lhsT=w_dealt[:, rows].bitcast(FP8X4),
-                    lhsT_scale=w_plane[:, rows],
+                    lhsT_scale=w_scale[:, rows],
                     rhs=z_codes[:, cols].bitcast(FP8X4),
                     rhs_scale=z_scale[:, cols],
                     start=True,
@@ -206,115 +218,84 @@ def tile_picked_hpqtwiceshare_none_po_kernel(
                 )
                 nc.scalar.activation(out=ex[:, t, cols], in_=h2_bank[:, :width], func=ACT.Exp, scale=0.5)
 
-        for t in range(PACK):
-            evacuate(t, 0)
-            evacuate(t, 1)
-            first_fetch(t, 0)
-            first_fetch(t, 1)
-            if t > 0:
-                subtract(t - 1)
-        subtract(PACK - 1)
-        for u in range(len(parts1)):
-            for t in range(PACK):
-                second_fetch(t, u)
-                combine(t, u)
-            weave_z(u)
-            second_product(u)
-
-        ex_n2 = {}
-        ex_n3 = {}
-        pair = keep.tile([P, PACK, S], F32)
-        total = keep.tile([P, PACK, S], F32)
         root = keep.tile([P, PACK, S], F32)
-        inverse = keep.tile([P, PACK, S], F32)
+        factor = keep.tile([P, PACK, S], F32)
         y = keep.tile([P, PACK, S], F32)
         y_woven = keep.tile([P, S, PACK], BF16, align_bytes=64)
         y_codes = keep.tile([P, S], U32, align_bytes=64)
         y_scale = keep.tile([P, S], U8, align_bytes=64)
         out_rows = out_0.rearrange("(p t) j -> p t j", t=PACK)
         out_words = as_words(out_1)
-        units = [(u, t, cols) for u, cols in enumerate([slice(0, 256), slice(256, 384), slice(384, 512)]) for t in range(PACK)]
-        sums = {}
-        back = {}
+        last_operands = {}
 
-        def on_pe(u, t):
-            return not (u == 2 and t >= 2)
-
-        def fetch(u, t, cols):
+        def share_by_transposes(part, t, ex_n2, ex_n3):
+            cols = PARTS[part]
             width = cols.stop - cols.start
-            ex_n2[u, t] = keep.tile([P, width], F32, name="ex_n2_%d%d" % (u, t), tag="ex_n2_%d" % t)
-            ex_n3[u, t] = keep.tile([P, width], F32, name="ex_n3_%d%d" % (u, t), tag="ex_n3_%d" % t)
-            gather("vector", ex_n2[u, t][:], ex[:, t, :], entries(n2_list, cols))
-            gather("scalar" if (u == 0 and t > 0) or u == 2 else "vector", ex_n3[u, t][:], ex[:, t, :], entries(n3_list, cols))
-
-        def add_first(u, t, cols):
-            if not on_pe(u, t):
-                nc.vector.tensor_tensor(out=pair[:, t, cols], in0=ex[:, t, cols], in1=ex_n2[u, t][:], op=ALU.add)
-
-        def add_second(u, t, cols):
-            if not on_pe(u, t):
-                nc.vector.tensor_tensor(out=total[:, t, cols], in0=pair[:, t, cols], in1=ex_n3[u, t][:], op=ALU.add)
-                return
-            width = cols.stop - cols.start
-            sums[u, t] = bank("sums%d%d" % (u, t), t)
-            terms = (ex[:, t, cols], ex_n2[u, t], ex_n3[u, t])
+            total = bank("total%d%d" % (part, t), t)
+            terms = (ex[:, t, cols], ex_n2, ex_n3)
             for j, term in enumerate(terms):
                 for c in range(0, width, P):
                     nc.tensor.matmul(
-                        sums[u, t][:, c : c + P], term[:, c : c + P], identity[:],
-                        start=(j == 0 and c == 0), stop=(j == 2 and c == width - P), is_transpose=True,
+                        total[:, c : c + P],
+                        term[:, c : c + P],
+                        identity[:],
+                        start=(j == 0 and c == 0),
+                        stop=(j == len(terms) - 1 and c == width - P),
+                        is_transpose=True,
                     )
-
-        def take_root(u, t, cols):
-            width = cols.stop - cols.start
-            src = sums[u, t][:, :width] if on_pe(u, t) else total[:, t, cols]
-            nc.scalar.activation(out=root[:, t, cols], in_=src, func=ACT.Abs_reciprocal_sqrt, scale=0.5)
-
-        def turn_back(u, t, cols, src):
-            width = cols.stop - cols.start
-            back[u, t] = bank("back%d%d" % (u, t), PACK + t)
+            nc.scalar.activation(
+                out=root[:, t, cols], in_=total[:, :width], func=ACT.Abs_reciprocal_sqrt, scale=0.5
+            )
+            nc.scalar.activation(out=factor[:, t, cols], in_=root[:, t, cols], func=ACT.Square)
+            turned_back = bank("turned_back%d%d" % (part, t), PACK + t)
             for c in range(0, width, P):
-                nc.tensor.transpose(back[u, t][:, c : c + P], src[:, t, cols.start + c : cols.start + c + P], identity[:])
+                nc.tensor.transpose(
+                    turned_back[:, c : c + P], factor[:, t, cols.start + c : cols.start + c + P], identity[:]
+                )
+            last_operands[part, t] = (ex[:, t, cols], turned_back[:, :width])
 
-        def square(u, t, cols):
+        def share_on_vector(part, t, ex_n2, ex_n3):
+            cols = PARTS[part]
             width = cols.stop - cols.start
-            if not (u == 2 and t >= 2):
-                nc.scalar.activation(out=inverse[:, t, cols], in_=root[:, t, cols], func=ACT.Square)
-                if on_pe(u, t):
-                    turn_back(u, t, cols, inverse)
-            else:
-                if on_pe(u, t):
-                    turn_back(u, t, cols, root)
-                src = back[u, t][:, :width] if on_pe(u, t) else root[:, t, cols]
-                nc.vector.tensor_tensor(out=inverse[:, t, cols], in0=ex[:, t, cols], in1=src, op=ALU.mult)
+            two_terms = keep.tile([P, width], F32, name="two_terms%d" % t)
+            three_terms = keep.tile([P, width], F32, name="three_terms%d" % t)
+            nc.vector.tensor_tensor(out=two_terms[:], in0=ex[:, t, cols], in1=ex_n2[:], op=ALU.add)
+            nc.vector.tensor_tensor(out=three_terms[:], in0=two_terms[:], in1=ex_n3[:], op=ALU.add)
+            nc.scalar.activation(out=root[:, t, cols], in_=three_terms[:], func=ACT.Abs_reciprocal_sqrt, scale=0.5)
+            nc.vector.tensor_tensor(out=factor[:, t, cols], in0=ex[:, t, cols], in1=root[:, t, cols], op=ALU.mult)
+            last_operands[part, t] = (factor[:, t, cols], root[:, t, cols])
 
-        def finish(u, t, cols):
+        def begin(part, t):
+            cols = PARTS[part]
             width = cols.stop - cols.start
-            if not (u == 2 and t >= 2):
-                src = back[u, t][:, :width] if on_pe(u, t) else inverse[:, t, cols]
-                nc.vector.tensor_tensor(out=y[:, t, cols], in0=ex[:, t, cols], in1=src, op=ALU.mult)
-            else:
-                src = back[u, t][:, :width] if on_pe(u, t) else root[:, t, cols]
-                nc.vector.tensor_tensor(out=y[:, t, cols], in0=inverse[:, t, cols], in1=src, op=ALU.mult)
+            ex_n2 = keep.tile([P, width], F32, name="ex_n2_%d%d" % (part, t), tag="ex_n2_%d" % t)
+            ex_n3 = keep.tile([P, width], F32, name="ex_n3_%d%d" % (part, t), tag="ex_n3_%d" % t)
+            vector_gather(ex_n2[:], ex[:, t, :], entries(n2_list, cols))
+            on_scalar = part == LAST_PART or (part == 0 and t > 0)
+            gather = scalar_gather if on_scalar else vector_gather
+            gather(ex_n3[:], ex[:, t, :], entries(n3_list, cols))
+            share = share_on_vector if (part == LAST_PART and t >= PACK - 2) else share_by_transposes
+            share(part, t, ex_n2, ex_n3)
+
+        def finish(part, t):
+            cols = PARTS[part]
+            in0, in1 = last_operands[part, t]
+            nc.vector.tensor_tensor(out=y[:, t, cols], in0=in0, in1=in1, op=ALU.mult)
             if t == PACK - 1:
                 nc.sync.dma_start(out_rows[:, :, cols], y[:, :, cols])
-                cut = cols.start + cols.stop - cols.start
-                if cut > cols.start:
-                    weave("vector", y_woven, y, slice(cols.start, cut))
-                if cut < cols.stop:
-                    weave("scalar", y_woven, y, slice(cut, cols.stop))
-                nc.vector.quantize_mx(
-                    out=y_codes[:, cols].bitcast(FP8X4),
-                    scales=y_scale[:, cols],
-                    in_=y_woven[:, cols, :].rearrange("p c t -> p (c t)"),
-                )
+                weave_and_quantize(y, y_woven, y_codes, y_scale, cols)
                 nc.sync.dma_start(out_words[:, cols], y_codes[:, cols].bitcast(I32))
 
-        stages = [(4, finish), (0, fetch), (0, add_first), (0, add_second), (0, take_root), (0, square)]
-        for step in range(len(units) + max(lag for lag, stage in stages)):
-            for lag, stage in stages:
-                if 0 <= step - lag < len(units):
-                    stage(*units[step - lag])
-        for q in range(4):
+        for part in range(len(PARTS) + 1):
+            for t in range(PACK):
+                if part > 0:
+                    finish(part - 1, t)
+                if part < len(PARTS):
+                    begin(part, t)
+
+        for q in range(P // QUADRANT):
             queue = nc.scalar if q % 2 == 0 else nc.sync
-            queue.dma_start(out_2[0, 4 * q : 4 * q + 4, :].bitcast(I32), y_scale[32 * q : 32 * q + 4, :].bitcast(I32))
+            queue.dma_start(
+                out_2[0, PACK * q : PACK * (q + 1), :].bitcast(I32),
+                y_scale[QUADRANT * q : QUADRANT * q + PACK, :].bitcast(I32),
+            )

from contextlib import ExitStack

import concourse.mybir as mybir
from concourse.masks import make_identity

K, T, S, N, G, H = 512, 2048, 512, 512, 2048, 512
FLOPS = 2 * K * H * S + 2 * H * N * S

F32 = mybir.dt.float32
BF16 = mybir.dt.bfloat16
I32 = mybir.dt.int32
U32 = mybir.dt.uint32
U16 = mybir.dt.uint16
U8 = mybir.dt.uint8
FP8X4 = mybir.dt.float8_e4m3fn_x4
ALU = mybir.AluOpType
ACT = mybir.ActivationFunctionType

P = 128
PACK = 4
GROUP = 16
QUADRANT = 32
BLOCKS = K // 32
BLOCK_PARTITIONS = P // BLOCKS
LINE = 4
HALF = S // 2
HALVES = [slice(0, HALF), slice(HALF, S)]
PARTS = [slice(0, 256), slice(256, 384), slice(384, 512)]
LAST_PART = len(PARTS) - 1


def tile_picked_hpqtwiceshare_none_po_kernel(
    tc, x_words, x_scales, d_words, d_scales, gn, w1_words, w1_scales, offs, k1, n1, n2, n3, out_0, out_1, out_2
):
    nc = tc.nc

    def entries(offsets, cols):
        return offsets[:, cols.start // GROUP : cols.stop // GROUP]

    def vector_gather(out, window, offsets):
        nc.vector.tensor_copy(out=out, in_=window.indirect(offsets))

    def scalar_gather(out, window, offsets):
        nc.scalar.activation(out=out, in_=window.indirect(offsets), func=ACT.Copy)

    def as_words(packed):
        return packed[0].rearrange("p n t -> p (n t)").bitcast(I32)

    def spread_rows(scales):
        scale_rows = scales[0].bitcast(I32)
        return scale_rows.unsqueeze(1).broadcast_to([BLOCKS, BLOCK_PARTITIONS, scale_rows.shape[1]])

    def dealt_words(dealt):
        return dealt.rearrange("p (t c i) -> p c t i", t=PACK, i=LINE)

    def plain_words(plain):
        return plain.rearrange("p (c i t) -> p c t i", t=PACK, i=LINE)

    def deal_bytes(dealt, plain):
        nc.vector.tensor_copy(
            out=dealt.rearrange("p (t m) -> p t m", t=PACK), in_=plain.rearrange("p (m t) -> p t m", t=PACK)
        )

    def weave_and_quantize(tiles, woven, codes, scales, cols):
        nc.vector.tensor_copy(
            out=woven[:, cols, :].rearrange("p (c i) t -> p c t i", i=LINE),
            in_=tiles[:, :, cols].rearrange("p t (c i) -> p c t i", i=LINE),
        )
        nc.vector.quantize_mx(
            out=codes[:, cols].bitcast(FP8X4),
            scales=scales[:, cols],
            in_=woven[:, cols, :].rearrange("p c t -> p (c t)"),
        )

    with ExitStack() as ctx:
        keep = ctx.enter_context(tc.tile_pool(name="keep", bufs=1))
        psum = ctx.enter_context(tc.psum_pool(name="psum", bufs=1))

        def bank(name, number):
            return psum.tile([P, S], F32, name=name, tag="bank%d" % number)

        k1_list = keep.tile([P, H // GROUP], U16)
        offs_list = keep.tile([P, S // GROUP], U16)
        n1_list = keep.tile([P, S // GROUP], U16)
        n2_list = keep.tile([P, S // GROUP], U16)
        n3_list = keep.tile([P, S // GROUP], U16)
        d_bytes = keep.tile([P, G], U8, align_bytes=64)
        x_bytes = keep.tile([P, T], U8, align_bytes=64)
        first_scales = keep.tile([P, H + S], U8, align_bytes=64)
        nc.gpsimd.memset(first_scales[:].bitcast(I32), 0)
        identity = keep.tile([P, P], F32)
        make_identity(nc, identity[:])
        nc.sync.dma_start(k1_list[:], k1)
        nc.sync.dma_start(d_bytes[:].bitcast(I32), spread_rows(d_scales))
        nc.sync.dma_start(offs_list[:], offs)
        nc.sync.dma_start(x_bytes[:].bitcast(I32), spread_rows(x_scales))

        d_table = keep.tile([P, G], U32, align_bytes=64, tag="d_table")
        x_table = keep.tile([P, T], U32, align_bytes=64, tag="x_table")
        gn_rows = keep.tile([P, PACK], F32)
        nc.sync.dma_start(d_table[:].bitcast(I32), as_words(d_words))
        nc.sync.dma_start(n1_list[:], n1)
        nc.sync.dma_start(n2_list[:], n2)
        nc.sync.dma_start(gn_rows[:], gn.rearrange("(p t) o -> p (t o)", t=PACK))
        nc.sync.dma_start(x_table[:].bitcast(I32), as_words(x_words))
        nc.sync.dma_start(n3_list[:], n3)
        gain = keep.tile([P, PACK], F32)
        nc.scalar.activation(out=gain[:], in_=gn_rows[:], func=ACT.Copy, scale=0.0625)

        d_bytes_picked = keep.tile([P, H], U8, align_bytes=64)
        x_bytes_picked = keep.tile([P, S], U8, align_bytes=64, tag="x_bytes_picked")
        vector_gather(d_bytes_picked[:], d_bytes[:], k1_list[:])
        vector_gather(x_bytes_picked[:], x_bytes[:], offs_list[:])
        joined = keep.tile([P, H + S], U8, align_bytes=64)
        deal_bytes(joined[:, :H], d_bytes_picked[:])
        nc.vector.tensor_copy(out=joined[:, H:].bitcast(I32), in_=x_bytes_picked[:].bitcast(I32))
        for r in range(PACK):
            nc.sync.dma_start(
                first_scales[r:P:QUADRANT, :].bitcast(I32),
                joined[BLOCK_PARTITIONS * r : P : QUADRANT, :].bitcast(I32),
            )
        w_table = keep.tile([P, N], U32, align_bytes=64, tag="x_bytes_picked")
        nc.sync.dma_start(w_table[:].bitcast(I32), as_words(w1_words))

        d_picked = keep.tile([P, H], U32, align_bytes=64)
        d_dealt = keep.tile([P, H], U32, align_bytes=64)
        x_picked = keep.tile([P, S], U32, align_bytes=64)
        vector_gather(d_picked[:], d_table[:], k1_list[:])
        nc.vector.tensor_copy(out=dealt_words(d_dealt[:]), in_=plain_words(d_picked[:]))
        for cols in HALVES:
            vector_gather(x_picked[:, cols], x_table[:], entries(offs_list, cols))

        w_bytes = keep.tile([P, N], U8, align_bytes=64, tag="d_table")
        for q in range(P // QUADRANT):
            scale_rows = w1_scales[0, PACK * q : PACK * (q + 1), :].bitcast(I32)
            nc.sync.dma_start(
                w_bytes[QUADRANT * q : QUADRANT * (q + 1), :].bitcast(I32),
                scale_rows.unsqueeze(0).broadcast_to([QUADRANT // PACK, PACK, scale_rows.shape[1]]),
            )
        w_dealt = keep.tile([P, N], U32, align_bytes=64)
        nc.scalar.copy(out=dealt_words(w_dealt[:]), in_=plain_words(w_table[:]))
        w_scale = keep.tile([P, N], U8, align_bytes=64, tag="x_table")
        deal_bytes(w_scale[:], w_bytes[:])

        h = [keep.tile([P, 2 * S], F32, name="h%d" % t, tag="h%d" % t) for t in range(PACK)]
        for t in range(PACK):
            clearing = nc.vector if t % 2 == 0 else nc.gpsimd
            clearing.memset(h[t][:, S:], 0.0)
        h_bank = {}
        for pair_of_tiles in ((0, 1), (2, 3)):
            for half, cols in enumerate(HALVES):
                for t in pair_of_tiles:
                    rows = slice(t * P, (t + 1) * P)
                    h_bank[half, t] = bank("h_bank%d%d" % (half, t), PACK * half + t)
                    nc.tensor.matmul_mx(
                        out=h_bank[half, t][:, :HALF],
                        lhsT=d_dealt[:, rows].bitcast(FP8X4),
                        lhsT_scale=first_scales[:, rows],
                        rhs=x_picked[:, cols].bitcast(FP8X4),
                        rhs_scale=first_scales[:, H + cols.start : H + cols.stop],
                        start=True,
                        stop=True,
                    )

        h_at = [keep.tile([P, S], F32, name="h_at%d" % t, tag="h_at%d" % t) for t in range(PACK)]
        st = [keep.tile([P, S], F32, name="st%d" % t) for t in range(PACK)]
        z_tiles = keep.tile([P, PACK, S], BF16, align_bytes=64)
        z_woven = keep.tile([P, S, PACK], BF16, align_bytes=64)
        z_codes = keep.tile([P, S], U32, align_bytes=64)
        z_scale = keep.tile([P, S], U8, align_bytes=64)
        ex = keep.tile([P, PACK, S], F32)

        def subtract(t):
            nc.vector.tensor_tensor(out=st[t][:], in0=h[t][:, :S], in1=h_at[t][:], op=ALU.subtract)

        for t in range(PACK):
            for half, cols in enumerate(HALVES):
                product = h_bank[half, t][:, :HALF]
                if t == 0:
                    nc.vector.tensor_scalar(h[t][:, cols], product, gain[:, t : t + 1], None, ALU.mult)
                else:
                    nc.scalar.activation(out=h[t][:, cols], in_=product, func=ACT.Copy, scale=gain[:, t : t + 1])
            gather = vector_gather if t % 2 == 0 else scalar_gather
            gather(h_at[t][:], h[t][:], n1_list[:])
            if t > 0:
                subtract(t - 1)
        subtract(PACK - 1)

        st_at_buffers = [("st_at0", "st_at2"), ("h_at3", "h3"), ("st_at0", "st_at2")]
        for part, cols in enumerate(PARTS):
            width = cols.stop - cols.start
            for t in range(PACK):
                if t % 2 == 0:
                    st_at = keep.tile(
                        [P, 2, width], F32, name="st_at%d%d" % (part, t), tag=st_at_buffers[part][t // 2]
                    )
                scalar_gather(st_at[:, t % 2, :], st[t][:], entries(n1_list, cols))
                nc.vector.scalar_tensor_tensor(
                    out=z_tiles[:, t, cols],
                    in0=st_at[:, t % 2, :],
                    scalar=-0.5,
                    in1=st[t][:, cols],
                    op0=ALU.mult,
                    op1=ALU.add,
                )
            weave_and_quantize(z_tiles, z_woven, z_codes, z_scale, cols)
            for t in range(PACK):
                rows = slice(t * P, (t + 1) * P)
                h2_bank = bank("h2_bank%d%d" % (part, t), PACK * (part % 2) + t)
                nc.tensor.matmul_mx(
                    out=h2_bank[:, :width],
                    lhsT=w_dealt[:, rows].bitcast(FP8X4),
                    lhsT_scale=w_scale[:, rows],
                    rhs=z_codes[:, cols].bitcast(FP8X4),
                    rhs_scale=z_scale[:, cols],
                    start=True,
                    stop=True,
                )
                nc.scalar.activation(out=ex[:, t, cols], in_=h2_bank[:, :width], func=ACT.Exp, scale=0.5)

        root = keep.tile([P, PACK, S], F32)
        factor = keep.tile([P, PACK, S], F32)
        y = keep.tile([P, PACK, S], F32)
        y_woven = keep.tile([P, S, PACK], BF16, align_bytes=64)
        y_codes = keep.tile([P, S], U32, align_bytes=64)
        y_scale = keep.tile([P, S], U8, align_bytes=64)
        out_rows = out_0.rearrange("(p t) j -> p t j", t=PACK)
        out_words = as_words(out_1)
        last_operands = {}

        def share_by_transposes(part, t, ex_n2, ex_n3):
            cols = PARTS[part]
            width = cols.stop - cols.start
            total = bank("total%d%d" % (part, t), t)
            terms = (ex[:, t, cols], ex_n2, ex_n3)
            for j, term in enumerate(terms):
                for c in range(0, width, P):
                    nc.tensor.matmul(
                        total[:, c : c + P],
                        term[:, c : c + P],
                        identity[:],
                        start=(j == 0 and c == 0),
                        stop=(j == len(terms) - 1 and c == width - P),
                        is_transpose=True,
                    )
            nc.scalar.activation(
                out=root[:, t, cols], in_=total[:, :width], func=ACT.Abs_reciprocal_sqrt, scale=0.5
            )
            nc.scalar.activation(out=factor[:, t, cols], in_=root[:, t, cols], func=ACT.Square)
            turned_back = bank("turned_back%d%d" % (part, t), PACK + t)
            for c in range(0, width, P):
                nc.tensor.transpose(
                    turned_back[:, c : c + P], factor[:, t, cols.start + c : cols.start + c + P], identity[:]
                )
            last_operands[part, t] = (ex[:, t, cols], turned_back[:, :width])

        def share_on_vector(part, t, ex_n2, ex_n3):
            cols = PARTS[part]
            width = cols.stop - cols.start
            two_terms = keep.tile([P, width], F32, name="two_terms%d" % t)
            three_terms = keep.tile([P, width], F32, name="three_terms%d" % t)
            nc.vector.tensor_tensor(out=two_terms[:], in0=ex[:, t, cols], in1=ex_n2[:], op=ALU.add)
            nc.vector.tensor_tensor(out=three_terms[:], in0=two_terms[:], in1=ex_n3[:], op=ALU.add)
            nc.scalar.activation(out=root[:, t, cols], in_=three_terms[:], func=ACT.Abs_reciprocal_sqrt, scale=0.5)
            nc.vector.tensor_tensor(out=factor[:, t, cols], in0=ex[:, t, cols], in1=root[:, t, cols], op=ALU.mult)
            last_operands[part, t] = (factor[:, t, cols], root[:, t, cols])

        def begin(part, t):
            cols = PARTS[part]
            width = cols.stop - cols.start
            ex_n2 = keep.tile([P, width], F32, name="ex_n2_%d%d" % (part, t), tag="ex_n2_%d" % t)
            ex_n3 = keep.tile([P, width], F32, name="ex_n3_%d%d" % (part, t), tag="ex_n3_%d" % t)
            vector_gather(ex_n2[:], ex[:, t, :], entries(n2_list, cols))
            on_scalar = part == LAST_PART or (part == 0 and t > 0)
            gather = scalar_gather if on_scalar else vector_gather
            gather(ex_n3[:], ex[:, t, :], entries(n3_list, cols))
            share = share_on_vector if (part == LAST_PART and t >= PACK - 2) else share_by_transposes
            share(part, t, ex_n2, ex_n3)

        def finish(part, t):
            cols = PARTS[part]
            in0, in1 = last_operands[part, t]
            nc.vector.tensor_tensor(out=y[:, t, cols], in0=in0, in1=in1, op=ALU.mult)
            if t == PACK - 1:
                nc.sync.dma_start(out_rows[:, :, cols], y[:, :, cols])
                weave_and_quantize(y, y_woven, y_codes, y_scale, cols)
                nc.sync.dma_start(out_words[:, cols], y_codes[:, cols].bitcast(I32))

        for part in range(len(PARTS) + 1):
            for t in range(PACK):
                if part > 0:
                    finish(part - 1, t)
                if part < len(PARTS):
                    begin(part, t)

        for q in range(P // QUADRANT):
            queue = nc.scalar if q % 2 == 0 else nc.sync
            queue.dma_start(
                out_2[0, PACK * q : PACK * (q + 1), :].bitcast(I32),
                y_scale[QUADRANT * q : QUADRANT * q + PACK, :].bitcast(I32),
            )
